import numpy as np
import ml_dtypes


def mxq(x, axis, fmt="e4m3"):
    dtype, down = {"e4m3": (ml_dtypes.float8_e4m3fn, 7), "e5m2": (ml_dtypes.float8_e5m2, 14)}[fmt]
    v = np.moveaxis(np.asarray(x, np.float32).astype(ml_dtypes.bfloat16).astype(np.float64), axis, -1)
    blocks = v.reshape(v.shape[:-1] + (-1, 32))
    amax = np.abs(blocks).max(-1, keepdims=True)
    byte = np.maximum(np.where(amax > 0, np.frexp(amax)[1] - 1 + 127, 0) - down, 1)
    scale = np.exp2(byte - 127.0)
    codes = (blocks / scale).astype(np.float32).astype(dtype).astype(np.float64)
    return np.moveaxis((codes * scale).reshape(v.shape), -1, axis)


WIDE = False


def mx_kscale(k):
    if not WIDE:
        return np.ones(k)
    levels = np.array([10, -10, 5, -5, 0])
    if k % 512:
        return np.exp2(np.random.permutation(np.resize(levels, k // 32))).repeat(32)
    a = np.empty((k // 512, 16))
    for p in range(k // 512):
        a[p, :8] = np.random.permutation(np.resize(levels, 8))
        for g in range(8):
            far = levels[np.abs(levels - a[p, g]) >= 10]
            a[p, g + 8] = far[np.random.randint(len(far))]
    return np.exp2(a.ravel()).repeat(32)


def f64(x):
    return np.asarray(x).astype(np.float64)


def striped(idx):
    return np.tile(idx.reshape(-1, 16).T, (8, 1)).astype(np.uint16)


def unstriped(offs):
    return offs[:16].T.reshape(-1).astype(np.int64)


K, T, D, S, V, N = 1024, 512, 4, 1024, 256, 256


def setup_inputs():
    n = np.random.standard_normal
    s = mx_kscale(K)[:, None]
    return {
        "xT": (n((K, T)) * s).astype(np.float32),
        "w": (n((K, N)) / np.sqrt(K) / s).astype(np.float32),
        "gate": np.tile(np.random.uniform(0.2, 1.0, (D, 1, V)) / np.sqrt(D), (1, N, 1)).astype(np.float32),
        "pos1": striped(np.random.permutation(T)[:V]),
        "pos2": striped(np.random.permutation(T)[:V]),
        "pos3": striped(np.random.permutation(T)[:V]),
        "pos4": striped(np.random.permutation(T)[:V]),
    }


def reference(xT, w, gate, pos1, pos2, pos3, pos4):
    y = mxq(f64(w), 0, "e4m3").T @ mxq(f64(xT), 0, "e4m3")
    return sum(f64(gate[d]) * y[:, unstriped(p)] for d, p in enumerate((pos1, pos2, pos3, pos4)))

from contextlib import ExitStack

import concourse.mybir as mybir

K, T, D, V, N = 1024, 512, 4, 256, 256
FLOPS = 2 * K * T * N + 2 * D * N * V

F32 = mybir.dt.float32
BF16 = mybir.dt.bfloat16
U32 = mybir.dt.uint32
U16 = mybir.dt.uint16
U8 = mybir.dt.uint8
FP8X4 = mybir.dt.float8_e4m3fn_x4
MULT = mybir.AluOpType.mult
ADD = mybir.AluOpType.add

P = 128
PACK = 4
PASSES = K // (P * PACK)
H = T // 2


def tile_picked_agg_lin_none_sub_l_kernel(tc, xT, w, gate, pos1, pos2, pos3, pos4, out):
    nc = tc.nc
    with ExitStack() as ctx:
        keep = ctx.enter_context(tc.tile_pool(name="keep", bufs=1))
        psum = ctx.enter_context(tc.psum_pool(name="psum", bufs=1))

        def quant_tiles(width, name):
            grouped = keep.tile([P, width, PACK], BF16, align_bytes=64, name="g_" + name)
            codes = keep.tile([P, width], U32, align_bytes=64, name="c_" + name)
            scales = keep.tile([P, width], U8, align_bytes=64, name="s_" + name)
            return grouped, codes, scales

        def cast(grouped, raw, width, cut):
            if cut > 0:
                nc.vector.tensor_copy(grouped[:, 0:cut, :], raw[:, :, 0:cut].rearrange("p j c -> p c j"))
            if cut < width:
                nc.scalar.copy(grouped[:, cut:width, :], raw[:, :, cut:width].rearrange("p j c -> p c j"))

        def quantize(q):
            nc.vector.quantize_mx(
                out=q[1][:].bitcast(FP8X4), scales=q[2][:], in_=q[0][:].rearrange("p c j -> p (c j)")
            )

        def multiply(bank, wq, xq, c):
            nc.tensor.matmul_mx(
                out=bank[:],
                lhsT=wq[1][:].bitcast(FP8X4),
                lhsT_scale=wq[2][:],
                rhs=xq[1][:].bitcast(FP8X4),
                rhs_scale=xq[2][:],
                start=(c == 0),
                stop=(c == PASSES - 1),
            )

        def rows(src, c):
            return src[c * 512 : (c + 1) * 512, :].rearrange("(p j) n -> p j n", j=PACK)

        lists = []
        for d in range(D):
            lists.append(keep.tile([P, V // 16], U16, name=f"pos{d}"))
        x_raw = [keep.tile([P, PACK, T], F32, name=f"x_raw{c}") for c in range(PASSES)]
        w_raw = [[keep.tile([P, PACK, P], F32, name=f"w_raw{m}{c}") for c in range(PASSES)] for m in range(2)]
        gates = [keep.tile([P, D, V], F32, name=f"gates{m}") for m in range(2)]

        def load_w(m, c):
            nc.sync.dma_start(out=w_raw[m][c][:], in_=rows(w, c)[:, :, m * P : (m + 1) * P])

        def load_x(c, h0, h1):
            nc.sync.dma_start(out=x_raw[c][:, :, h0:h1], in_=rows(xT, c)[:, :, h0:h1])

        def load_gate(m, d0, d1):
            nc.sync.dma_start(
                out=gates[m][:, d0:d1, :], in_=gate[d0:d1, m * P : (m + 1) * P, :].rearrange("d p v -> p d v")
            )

        load_x(0, 0, H)
        load_x(0, H, T)
        load_w(0, 0)
        load_x(1, 0, H)
        load_x(1, H, T)
        load_w(0, 1)
        nc.sync.dma_start(out=lists[0][:], in_=pos1)
        load_gate(0, 0, 2)
        nc.sync.dma_start(out=lists[1][:], in_=pos2)
        load_w(1, 0)
        load_w(1, 1)
        nc.sync.dma_start(out=lists[2][:], in_=pos3)
        nc.sync.dma_start(out=lists[3][:], in_=pos4)
        load_gate(0, 2, 4)
        load_gate(1, 0, 4)

        xq = [[quant_tiles(H, f"x{c}{h}") for h in range(2)] for c in range(PASSES)]
        wq = [[quant_tiles(P, f"w0{c}") for c in range(PASSES)]]
        late = quant_tiles(PASSES * P, "w1")
        wq.append([[t[:, c * P : (c + 1) * P] for t in late] for c in range(PASSES)])
        banks = [[psum.tile([P, H], F32, name=f"bank{m}{h}") for h in range(2)] for m in range(2)]
        y = [keep.tile([P, T], F32, name=f"y{m}") for m in range(2)]
        prod = [keep.tile([P, D, V], F32, name=f"prod{m}") for m in range(2)]
        part = [keep.tile([P, 2, V], F32, name=f"part{m}") for m in range(2)]
        res = [keep.tile([P, V], F32, name=f"res{m}") for m in range(2)]

        XCUT, WCUT = 128, 80
        for c in range(PASSES):
            for h in range(2):
                cast(xq[c][h][0], x_raw[c][:, :, h * H : (h + 1) * H], H, XCUT)
                quantize(xq[c][h])
            cast(wq[0][c][0], w_raw[0][c], P, WCUT)
            quantize(wq[0][c])
            for h in range(2):
                multiply(banks[0][h], wq[0][c], xq[c][h], c)
        nc.scalar.copy(y[0][:, 0:H], banks[0][0][:])
        nc.vector.tensor_copy(y[0][:, H:T], banks[0][1][:])

        def gather(m, d, v0, v1):
            nc.vector.tensor_tensor(
                prod[m][:, d, v0:v1],
                y[m][:].indirect(lists[d][:, v0 // 16 : v1 // 16]),
                gates[m][:, d, v0:v1],
                MULT,
            )

        for c in range(PASSES):
            nc.scalar.copy(late[0][:, c * P : (c + 1) * P, :], w_raw[1][c][:].rearrange("p j c -> p c j"))
        gather(0, 0, 0, V)
        gather(0, 1, 0, V)
        quantize(late)
        for c in range(PASSES):
            for h in range(2):
                multiply(banks[1][h], wq[1][c], xq[c][h], c)
        for h in range(2):
            nc.scalar.copy(y[1][:, h * H : (h + 1) * H], banks[1][h][:])
        gather(0, 2, 0, V)
        gather(0, 3, 0, V)
        gather(1, 0, 0, V)
        nc.vector.tensor_tensor(part[0][:], prod[0][:, 0:2, :], prod[0][:, 2:4, :], ADD)
        gather(1, 1, 0, V)
        nc.vector.tensor_tensor(res[0][:], part[0][:, 0, :], part[0][:, 1, :], ADD)
        nc.sync.dma_start(out=out[0:P, :], in_=res[0][:])
        gather(1, 2, 0, V)
        half = V // 2
        nc.vector.tensor_tensor(part[1][:, 0, :], prod[1][:, 0, :], prod[1][:, 1, :], ADD)
        gather(1, 3, 0, half)
        nc.vector.tensor_tensor(part[1][:, 1, :], part[1][:, 0, :], prod[1][:, 2, :], ADD)
        gather(1, 3, half, V)
        nc.vector.tensor_tensor(res[1][:, 0:half], part[1][:, 1, 0:half], prod[1][:, 3, 0:half], ADD)
        nc.sync.dma_start(out=out[P : 2 * P, 0:half], in_=res[1][:, 0:half])
        nc.vector.tensor_tensor(res[1][:, half:V], part[1][:, 1, half:V], prod[1][:, 3, half:V], ADD)
        nc.sync.dma_start(out=out[P : 2 * P, half:V], in_=res[1][:, half:V])
